import numpy as np
import ml_dtypes


def mxq(x, axis, fmt="e4m3"):
    dtype, down = {"e4m3": (ml_dtypes.float8_e4m3fn, 7), "e5m2": (ml_dtypes.float8_e5m2, 14)}[fmt]
    v = np.moveaxis(np.asarray(x, np.float32).astype(ml_dtypes.bfloat16).astype(np.float64), axis, -1)
    blocks = v.reshape(v.shape[:-1] + (-1, 32))
    amax = np.abs(blocks).max(-1, keepdims=True)
    byte = np.maximum(np.where(amax > 0, np.frexp(amax)[1] - 1 + 127, 0) - down, 1)
    scale = np.exp2(byte - 127.0)
    codes = (blocks / scale).astype(np.float32).astype(dtype).astype(np.float64)
    return np.moveaxis((codes * scale).reshape(v.shape), -1, axis)


WIDE = False


def mx_kscale(k):
    if not WIDE:
        return np.ones(k)
    levels = np.array([10, -10, 5, -5, 0])
    if k % 512:
        return np.exp2(np.random.permutation(np.resize(levels, k // 32))).repeat(32)
    a = np.empty((k // 512, 16))
    for p in range(k // 512):
        a[p, :8] = np.random.permutation(np.resize(levels, 8))
        for g in range(8):
            far = levels[np.abs(levels - a[p, g]) >= 10]
            a[p, g + 8] = far[np.random.randint(len(far))]
    return np.exp2(a.ravel()).repeat(32)


def f64(x):
    return np.asarray(x).astype(np.float64)


def striped(idx):
    return np.tile(idx.reshape(-1, 16).T, (8, 1)).astype(np.uint16)


def unstriped(offs):
    return offs[:16].T.reshape(-1).astype(np.int64)


def pack_weight(w):
    k, n = w.shape
    w = f64(np.asarray(w, np.float32).astype(ml_dtypes.bfloat16)).reshape(k // 32, 32, n)
    amax = np.abs(w).max(1)
    byte = np.clip(np.where(amax > 0, np.frexp(amax)[1] - 1 + 127 - 7, 1), 1, 254)
    scaled = (w * np.exp2(127.0 - byte)[:, None, :]).reshape(k, n).astype(np.float32)
    words = np.ascontiguousarray(scaled.reshape(k // 512, 128, 4, n).transpose(0, 1, 3, 2)).astype(ml_dtypes.float8_e4m3fn).view(np.uint8)
    return words, np.ascontiguousarray(byte.astype(np.uint8).reshape(k // 512, 16, n))


def unpack_weight(words, scales):
    g, p, n, _ = words.shape
    vals = np.ascontiguousarray(words).view(ml_dtypes.float8_e4m3fn).astype(np.float64) * np.repeat(np.exp2(scales.astype(np.float64) - 127.0), 8, axis=1)[..., None]
    return vals.transpose(0, 1, 3, 2).reshape(g * 512, n)


def sigmoid(v):
    return 1.0 / (1.0 + np.exp(-np.maximum(v, -700.0)))


K, T, S, V, N = 1024, 1024, 512, 256, 256


def setup_inputs():
    n = np.random.standard_normal
    s = mx_kscale(K)[:, None]
    packed_xT = pack_weight(n((K, T)) * s)
    return {
        "x_words": packed_xT[0],
        "x_scales": packed_xT[1],
        "w1": (n((K, N)) / np.sqrt(K) / s).astype(np.float32),
        "offs": striped(np.random.permutation(T)[:S]),
        "win": striped(np.random.permutation(S)[:V]),
        "lose": striped(np.random.permutation(S)[:V]),
    }


def reference(x_words, x_scales, w1, offs, win, lose):
    xq = unpack_weight(x_words, x_scales)[:, unstriped(offs)]
    y = mxq(f64(w1), 0, "e4m3").T @ xq
    return sigmoid(y[:, unstriped(win)] - y[:, unstriped(lose)])

@@ -1,0 +1,151 @@
+from contextlib import ExitStack
+
+import concourse.mybir as mybir
+
+K, T, S, V, N = 1024, 1024, 512, 256, 256
+FLOPS = 2 * K * S * N
+
+F32 = mybir.dt.float32
+BF16 = mybir.dt.bfloat16
+I32 = mybir.dt.int32
+U32 = mybir.dt.uint32
+U16 = mybir.dt.uint16
+U8 = mybir.dt.uint8
+FP8X4 = mybir.dt.float8_e4m3fn_x4
+SIGMOID = mybir.ActivationFunctionType.Sigmoid
+SUBTRACT = mybir.AluOpType.subtract
+
+P = 128
+PACK = 4
+PASSES = 2
+HALF = S // 2
+
+
+def tile_picked_ranknet_sigmoid_p_kernel(tc, x_words, x_scales, w1, offs, win, lose, out):
+    nc = tc.nc
+    with ExitStack() as ctx:
+        pool = ctx.enter_context(tc.tile_pool(name="pool", bufs=1))
+        psum = ctx.enter_context(tc.psum_pool(name="psum", bufs=1))
+
+        offs_t = pool.tile([P, S // 16], U16, name="offs_t")
+        win_t = pool.tile([P, V // 16], U16, name="win_t")
+        lose_t = pool.tile([P, V // 16], U16, name="lose_t")
+        xs = pool.tile([P, T], U8, name="xs", align_bytes=64)
+        xw = [pool.tile([P, T], I32, name=f"xw{z}", align_bytes=64) for z in range(PASSES)]
+        wraw = {(b, z): pool.tile([P, PACK, P], F32, name=f"wraw{b}{z}", align_bytes=64) for b in range(2) for z in range(PASSES)}
+        wbf = {(b, z): pool.tile([P, P * PACK], BF16, name=f"wbf{b}{z}", align_bytes=64) for b in range(2) for z in range(PASSES)}
+        wq = {(b, z): pool.tile([P, P], U32, name=f"wq{b}{z}", align_bytes=64) for b in range(2) for z in range(PASSES)}
+        ws = {(b, z): pool.tile([P, P], U8, name=f"ws{b}{z}", align_bytes=64) for b in range(2) for z in range(PASSES)}
+        gs = pool.tile([P, S], U8, name="gs", align_bytes=64)
+        gw = {(z, h): pool.tile([P, HALF], U32, name=f"gw{z}{h}", align_bytes=64) for z in range(PASSES) for h in range(2)}
+        acc = {(b, h): psum.tile([P, HALF], F32, name=f"acc{b}{h}") for b in range(2) for h in range(2)}
+        y = [pool.tile([P, S], F32, name=f"y{b}", align_bytes=64) for b in range(2)]
+        warm = pool.tile([P, 8], F32, name="warm")
+        warm2 = pool.tile([P, 8], F32, name="warm2")
+
+        def load_w(b, z, eng):
+            eng.dma_start(out=wraw[b, z][:], in_=w1[512 * z : 512 * (z + 1), P * b : P * (b + 1)].rearrange("(p j) m -> p j m", j=PACK))
+
+        def load_x(z, eng):
+            eng.dma_start(out=xw[z][:], in_=x_words[z].rearrange("p n t -> p (n t)").bitcast(I32))
+
+        def load_s(q, eng):
+            eng.dma_start(out=xs[32 * q : 32 * q + 8, :].bitcast(I32), in_=x_scales[:, 4 * q : 4 * q + 4, :].bitcast(I32))
+
+        def cast(b, z, eng):
+            dst = wbf[b, z][:].rearrange("p (c i t) -> p c t i", i=4, t=PACK)
+            src = wraw[b, z][:].rearrange("p t (c i) -> p c t i", i=4)
+            if eng == "v":
+                nc.vector.tensor_copy(out=dst, in_=src)
+            else:
+                nc.scalar.copy(out=dst, in_=src)
+
+        def quant(b, z):
+            nc.vector.quantize_mx(out=wq[b, z][:].bitcast(FP8X4), scales=ws[b, z][:], in_=wbf[b, z][:])
+
+        def gather_x(z, h):
+            nc.vector.tensor_copy(out=gw[z, h][:], in_=xw[z][:].bitcast(U32).indirect(offs_t[:, 16 * h : 16 * (h + 1)]))
+
+        def mm(b, h, z):
+            nc.tensor.matmul_mx(
+                out=acc[b, h][:],
+                lhsT=wq[b, z][:].bitcast(FP8X4),
+                lhsT_scale=ws[b, z][:],
+                rhs=gw[z, h][:].bitcast(FP8X4),
+                rhs_scale=gs[4 * z : P, HALF * h : HALF * (h + 1)],
+                start=(z == 0),
+                stop=(z == PASSES - 1),
+            )
+
+        def evac(b, h, eng):
+            if eng == "v":
+                nc.vector.tensor_copy(out=y[b][:, HALF * h : HALF * (h + 1)], in_=acc[b, h][:])
+            else:
+                nc.scalar.copy(out=y[b][:, HALF * h : HALF * (h + 1)], in_=acc[b, h][:])
+
+        low = {}
+        dif = {}
+
+        def g_lose(b, c0, c1):
+            low[b, c0] = pool.tile([P, c1 - c0], F32, name=f"low{b}{c0}")
+            nc.vector.tensor_copy(out=low[b, c0][:], in_=y[b][:].indirect(lose_t[:, c0 // 16 : c1 // 16]))
+
+        def g_win(b, c0, c1):
+            dif[b, c0] = pool.tile([P, c1 - c0], F32, name=f"dif{b}{c0}")
+            nc.vector.tensor_tensor(out=dif[b, c0][:], in0=y[b][:].indirect(win_t[:, c0 // 16 : c1 // 16]), in1=low[b, c0][:], op=SUBTRACT)
+
+        def finish(b, c0, c1, eng):
+            res = pool.tile([P, c1 - c0], F32, name=f"res{b}{c0}")
+            nc.scalar.activation(out=res[:], in_=dif[b, c0][:], func=SIGMOID)
+            eng.dma_start(out=out[P * b : P * (b + 1), c0:c1], in_=res[:])
+
+        nc.vector.memset(xs[:].bitcast(I32), 0)
+        nc.vector.memset(warm[:], 0.0)
+        nc.sync.dma_start(out=offs_t[:], in_=offs)
+        load_s(0, nc.scalar)
+        load_s(1, nc.scalar)
+        load_s(2, nc.scalar)
+        load_s(3, nc.scalar)
+        nc.scalar.activation(out=warm2[:], in_=warm[:], func=SIGMOID)
+        load_w(0, 0, nc.sync)
+        load_w(0, 1, nc.sync)
+        load_x(0, nc.sync)
+        load_x(1, nc.sync)
+        load_w(1, 0, nc.sync)
+        load_w(1, 1, nc.sync)
+        nc.sync.dma_start(out=lose_t[:], in_=lose)
+        nc.sync.dma_start(out=win_t[:], in_=win)
+        nc.vector.tensor_copy(out=gs[:], in_=xs[:].indirect(offs_t[:]))
+        cast(0, 0, "s")
+        cast(0, 1, "s")
+        quant(0, 0)
+        gather_x(0, 0)
+        quant(0, 1)
+        gather_x(0, 1)
+        mm(0, 0, 0)
+        mm(0, 1, 0)
+        gather_x(1, 0)
+        mm(0, 0, 1)
+        gather_x(1, 1)
+        mm(0, 1, 1)
+        evac(0, 0, "s")
+        cast(1, 0, "v")
+        cast(1, 1, "v")
+        evac(0, 1, "s")
+        quant(1, 0)
+        quant(1, 1)
+        mm(1, 0, 0)
+        mm(1, 0, 1)
+        mm(1, 1, 0)
+        mm(1, 1, 1)
+        g_lose(0, 0, 256)
+        evac(1, 0, "s")
+        evac(1, 1, "s")
+        g_win(0, 0, 256)
+        finish(0, 0, 256, nc.sync)
+        g_lose(1, 0, 128)
+        g_lose(1, 128, 256)
+        g_win(1, 0, 128)
+        finish(1, 0, 128, nc.sync)
+        g_win(1, 128, 256)
+        finish(1, 128, 256, nc.sync)

@@ -33,11 +33,11 @@ def tile_picked_ranknet_sigmoid_p_kernel(tc, x_words, x_scales, w1, offs, win, l
         xs = pool.tile([P, T], U8, name="xs", align_bytes=64)
         xw = [pool.tile([P, T], I32, name=f"xw{z}", align_bytes=64) for z in range(PASSES)]
         wraw = {(b, z): pool.tile([P, PACK, P], F32, name=f"wraw{b}{z}", align_bytes=64) for b in range(2) for z in range(PASSES)}
-        wbf = {(b, z): pool.tile([P, P * PACK], BF16, name=f"wbf{b}{z}", align_bytes=64) for b in range(2) for z in range(PASSES)}
-        wq = {(b, z): pool.tile([P, P], U32, name=f"wq{b}{z}", align_bytes=64) for b in range(2) for z in range(PASSES)}
-        ws = {(b, z): pool.tile([P, P], U8, name=f"ws{b}{z}", align_bytes=64) for b in range(2) for z in range(PASSES)}
+        wbf = [pool.tile([P, PASSES, P * PACK], BF16, name=f"wbf{b}", align_bytes=64) for b in range(2)]
+        wq = [pool.tile([P, PASSES, P], U32, name=f"wq{b}", align_bytes=64) for b in range(2)]
+        ws = [pool.tile([P, PASSES, P], U8, name=f"ws{b}", align_bytes=64) for b in range(2)]
         gs = pool.tile([P, S], U8, name="gs", align_bytes=64)
-        gw = {(z, h): pool.tile([P, HALF], U32, name=f"gw{z}{h}", align_bytes=64) for z in range(PASSES) for h in range(2)}
+        gw = [pool.tile([P, S], U32, name=f"gw{z}", align_bytes=64) for z in range(PASSES)]
         acc = {(b, h): psum.tile([P, HALF], F32, name=f"acc{b}{h}") for b in range(2) for h in range(2)}
         y = [pool.tile([P, S], F32, name=f"y{b}", align_bytes=64) for b in range(2)]
         warm = pool.tile([P, 8], F32, name="warm")
@@ -53,25 +53,29 @@ def tile_picked_ranknet_sigmoid_p_kernel(tc, x_words, x_scales, w1, offs, win, l
             eng.dma_start(out=xs[32 * q : 32 * q + 8, :].bitcast(I32), in_=x_scales[:, 4 * q : 4 * q + 4, :].bitcast(I32))
 
         def cast(b, z, eng):
-            dst = wbf[b, z][:].rearrange("p (c i t) -> p c t i", i=4, t=PACK)
+            dst = wbf[b][:, z, :].rearrange("p (c i t) -> p c t i", i=4, t=PACK)
             src = wraw[b, z][:].rearrange("p t (c i) -> p c t i", i=4)
             if eng == "v":
                 nc.vector.tensor_copy(out=dst, in_=src)
             else:
                 nc.scalar.copy(out=dst, in_=src)
 
-        def quant(b, z):
-            nc.vector.quantize_mx(out=wq[b, z][:].bitcast(FP8X4), scales=ws[b, z][:], in_=wbf[b, z][:])
+        def quant(b, z0, z1):
+            nc.vector.quantize_mx(
+                out=wq[b][:, z0:z1, :].rearrange("p z m -> p (z m)").bitcast(FP8X4),
+                scales=ws[b][:, z0:z1, :].rearrange("p z m -> p (z m)"),
+                in_=wbf[b][:, z0:z1, :].rearrange("p z m -> p (z m)"),
+            )
 
-        def gather_x(z, h):
-            nc.vector.tensor_copy(out=gw[z, h][:], in_=xw[z][:].bitcast(U32).indirect(offs_t[:, 16 * h : 16 * (h + 1)]))
+        def gather_x(z, c0, c1):
+            nc.vector.tensor_copy(out=gw[z][:, c0:c1], in_=xw[z][:].bitcast(U32).indirect(offs_t[:, c0 // 16 : c1 // 16]))
 
         def mm(b, h, z):
             nc.tensor.matmul_mx(
                 out=acc[b, h][:],
-                lhsT=wq[b, z][:].bitcast(FP8X4),
-                lhsT_scale=ws[b, z][:],
-                rhs=gw[z, h][:].bitcast(FP8X4),
+                lhsT=wq[b][:, z, :].bitcast(FP8X4),
+                lhsT_scale=ws[b][:, z, :],
+                rhs=gw[z][:, HALF * h : HALF * (h + 1)].bitcast(FP8X4),
                 rhs_scale=gs[4 * z : P, HALF * h : HALF * (h + 1)],
                 start=(z == 0),
                 stop=(z == PASSES - 1),
@@ -83,33 +87,31 @@ def tile_picked_ranknet_sigmoid_p_kernel(tc, x_words, x_scales, w1, offs, win, l
             else:
                 nc.scalar.copy(out=y[b][:, HALF * h : HALF * (h + 1)], in_=acc[b, h][:])
 
-        low = {}
-        dif = {}
+        low = [pool.tile([P, V], F32, name=f"low{b}") for b in range(2)]
+        dif = [pool.tile([P, V], F32, name=f"dif{b}") for b in range(2)]
 
         def g_lose(b, c0, c1):
-            low[b, c0] = pool.tile([P, c1 - c0], F32, name=f"low{b}{c0}")
-            nc.vector.tensor_copy(out=low[b, c0][:], in_=y[b][:].indirect(lose_t[:, c0 // 16 : c1 // 16]))
+            nc.vector.tensor_copy(out=low[b][:, c0:c1], in_=y[b][:].indirect(lose_t[:, c0 // 16 : c1 // 16]))
 
         def g_win(b, c0, c1):
-            dif[b, c0] = pool.tile([P, c1 - c0], F32, name=f"dif{b}{c0}")
-            nc.vector.tensor_tensor(out=dif[b, c0][:], in0=y[b][:].indirect(win_t[:, c0 // 16 : c1 // 16]), in1=low[b, c0][:], op=SUBTRACT)
+            nc.vector.tensor_tensor(out=dif[b][:, c0:c1], in0=y[b][:].indirect(win_t[:, c0 // 16 : c1 // 16]), in1=low[b][:, c0:c1], op=SUBTRACT)
 
         def finish(b, c0, c1, eng):
             res = pool.tile([P, c1 - c0], F32, name=f"res{b}{c0}")
-            nc.scalar.activation(out=res[:], in_=dif[b, c0][:], func=SIGMOID)
+            nc.scalar.activation(out=res[:], in_=dif[b][:, c0:c1], func=SIGMOID)
             eng.dma_start(out=out[P * b : P * (b + 1), c0:c1], in_=res[:])
 
         nc.vector.memset(xs[:].bitcast(I32), 0)
         nc.vector.memset(warm[:], 0.0)
-        nc.sync.dma_start(out=offs_t[:], in_=offs)
-        load_s(0, nc.scalar)
-        load_s(1, nc.scalar)
-        load_s(2, nc.scalar)
-        load_s(3, nc.scalar)
-        nc.scalar.activation(out=warm2[:], in_=warm[:], func=SIGMOID)
         load_w(0, 0, nc.sync)
-        load_w(0, 1, nc.sync)
+        nc.sync.dma_start(out=offs_t[:], in_=offs)
+        load_s(0, nc.sync)
+        load_s(1, nc.sync)
+        load_s(2, nc.sync)
+        load_s(3, nc.sync)
+        nc.scalar.activation(out=warm2[:], in_=warm[:], func=SIGMOID)
         load_x(0, nc.sync)
+        load_w(0, 1, nc.sync)
         load_x(1, nc.sync)
         load_w(1, 0, nc.sync)
         load_w(1, 1, nc.sync)
@@ -118,30 +120,30 @@ def tile_picked_ranknet_sigmoid_p_kernel(tc, x_words, x_scales, w1, offs, win, l
         nc.vector.tensor_copy(out=gs[:], in_=xs[:].indirect(offs_t[:]))
         cast(0, 0, "s")
         cast(0, 1, "s")
-        quant(0, 0)
-        gather_x(0, 0)
-        quant(0, 1)
-        gather_x(0, 1)
+        gather_x(0, 0, 512)
+        quant(0, 0, 2)
         mm(0, 0, 0)
         mm(0, 1, 0)
-        gather_x(1, 0)
+        gather_x(1, 0, 256)
         mm(0, 0, 1)
-        gather_x(1, 1)
+        gather_x(1, 256, 512)
         mm(0, 1, 1)
+        cast(1, 0, "s")
         evac(0, 0, "s")
-        cast(1, 0, "v")
         cast(1, 1, "v")
         evac(0, 1, "s")
-        quant(1, 0)
-        quant(1, 1)
+        quant(1, 0, 1)
+        quant(1, 1, 2)
         mm(1, 0, 0)
-        mm(1, 0, 1)
         mm(1, 1, 0)
+        mm(1, 0, 1)
         mm(1, 1, 1)
-        g_lose(0, 0, 256)
+        g_lose(0, 0, 128)
+        g_lose(0, 128, 256)
         evac(1, 0, "s")
         evac(1, 1, "s")
-        g_win(0, 0, 256)
+        g_win(0, 0, 128)
+        g_win(0, 128, 256)
         finish(0, 0, 256, nc.sync)
         g_lose(1, 0, 128)
         g_lose(1, 128, 256)

@@ -18,7 +18,6 @@ SUBTRACT = mybir.AluOpType.subtract
 P = 128
 PACK = 4
 PASSES = 2
-HALF = S // 2
 
 
 def tile_picked_ranknet_sigmoid_p_kernel(tc, x_words, x_scales, w1, offs, win, lose, out):
@@ -32,19 +31,23 @@ def tile_picked_ranknet_sigmoid_p_kernel(tc, x_words, x_scales, w1, offs, win, l
         lose_t = pool.tile([P, V // 16], U16, name="lose_t")
         xs = pool.tile([P, T], U8, name="xs", align_bytes=64)
         xw = [pool.tile([P, T], I32, name=f"xw{z}", align_bytes=64) for z in range(PASSES)]
-        wraw = {(b, z): pool.tile([P, PACK, P], F32, name=f"wraw{b}{z}", align_bytes=64) for b in range(2) for z in range(PASSES)}
-        wbf = [pool.tile([P, PASSES, P * PACK], BF16, name=f"wbf{b}", align_bytes=64) for b in range(2)]
-        wq = [pool.tile([P, PASSES, P], U32, name=f"wq{b}", align_bytes=64) for b in range(2)]
-        ws = [pool.tile([P, PASSES, P], U8, name=f"ws{b}", align_bytes=64) for b in range(2)]
+        wbf = [pool.tile([P, PASSES * P * PACK], BF16, name=f"wbf{b}", align_bytes=64) for b in range(2)]
+        wq = [pool.tile([P, PASSES * P], U32, name=f"wq{b}", align_bytes=64) for b in range(2)]
+        ws = [pool.tile([P, PASSES * P], U8, name=f"ws{b}", align_bytes=64) for b in range(2)]
         gs = pool.tile([P, S], U8, name="gs", align_bytes=64)
         gw = [pool.tile([P, S], U32, name=f"gw{z}", align_bytes=64) for z in range(PASSES)]
-        acc = {(b, h): psum.tile([P, HALF], F32, name=f"acc{b}{h}") for b in range(2) for h in range(2)}
         y = [pool.tile([P, S], F32, name=f"y{b}", align_bytes=64) for b in range(2)]
+        low = [pool.tile([P, V], F32, name=f"low{b}") for b in range(2)]
+        dif = [pool.tile([P, V], F32, name=f"dif{b}") for b in range(2)]
         warm = pool.tile([P, 8], F32, name="warm")
         warm2 = pool.tile([P, 8], F32, name="warm2")
+        wraw = []
+        acc = {}
 
-        def load_w(b, z, eng):
-            eng.dma_start(out=wraw[b, z][:], in_=w1[512 * z : 512 * (z + 1), P * b : P * (b + 1)].rearrange("(p j) m -> p j m", j=PACK))
+        def load_w(z, m0, m1, eng):
+            raw = pool.tile([P, PACK, m1 - m0], F32, name=f"wraw{z}_{m0}", align_bytes=64)
+            wraw.append((z, m0, m1, raw))
+            eng.dma_start(out=raw[:], in_=w1[512 * z : 512 * (z + 1), m0:m1].rearrange("(p j) m -> p j m", j=PACK))
 
         def load_x(z, eng):
             eng.dma_start(out=xw[z][:], in_=x_words[z].rearrange("p n t -> p (n t)").bitcast(I32))
@@ -52,43 +55,47 @@ def tile_picked_ranknet_sigmoid_p_kernel(tc, x_words, x_scales, w1, offs, win, l
         def load_s(q, eng):
             eng.dma_start(out=xs[32 * q : 32 * q + 8, :].bitcast(I32), in_=x_scales[:, 4 * q : 4 * q + 4, :].bitcast(I32))
 
-        def cast(b, z, eng):
-            dst = wbf[b][:, z, :].rearrange("p (c i t) -> p c t i", i=4, t=PACK)
-            src = wraw[b, z][:].rearrange("p t (c i) -> p c t i", i=4)
+        def cast(z, m0, m1, eng):
+            zz, a, b, raw = [w for w in wraw if w[0] == z and w[1] <= m0 and m1 <= w[2]][0]
+            c0 = P * z + m0 % P
+            dst = wbf[m0 // P][:, PACK * c0 : PACK * (c0 + m1 - m0)].rearrange("p (c i t) -> p c t i", i=4, t=PACK)
+            src = raw[:, :, m0 - a : m1 - a].rearrange("p t (c i) -> p c t i", i=4)
             if eng == "v":
                 nc.vector.tensor_copy(out=dst, in_=src)
+            elif eng == "g":
+                nc.gpsimd.tensor_copy(out=dst, in_=src)
             else:
                 nc.scalar.copy(out=dst, in_=src)
 
         def quant(b, z0, z1):
-            nc.vector.quantize_mx(
-                out=wq[b][:, z0:z1, :].rearrange("p z m -> p (z m)").bitcast(FP8X4),
-                scales=ws[b][:, z0:z1, :].rearrange("p z m -> p (z m)"),
-                in_=wbf[b][:, z0:z1, :].rearrange("p z m -> p (z m)"),
-            )
+            nc.vector.quantize_mx(out=wq[b][:, P * z0 : P * z1].bitcast(FP8X4), scales=ws[b][:, P * z0 : P * z1], in_=wbf[b][:, PACK * P * z0 : PACK * P * z1])
+
+        def gather_s(c0, c1):
+            nc.vector.tensor_copy(out=gs[:, c0:c1], in_=xs[:].indirect(offs_t[:, c0 // 16 : c1 // 16]))
 
         def gather_x(z, c0, c1):
             nc.vector.tensor_copy(out=gw[z][:, c0:c1], in_=xw[z][:].bitcast(U32).indirect(offs_t[:, c0 // 16 : c1 // 16]))
 
-        def mm(b, h, z):
+        def mm(b, c0, c1, z, first):
+            if first:
+                acc[b, c0] = psum.tile([P, c1 - c0], F32, name=f"acc{b}_{c0}")
             nc.tensor.matmul_mx(
-                out=acc[b, h][:],
-                lhsT=wq[b][:, z, :].bitcast(FP8X4),
-                lhsT_scale=ws[b][:, z, :],
-                rhs=gw[z][:, HALF * h : HALF * (h + 1)].bitcast(FP8X4),
-                rhs_scale=gs[4 * z : P, HALF * h : HALF * (h + 1)],
-                start=(z == 0),
-                stop=(z == PASSES - 1),
+                out=acc[b, c0][:],
+                lhsT=wq[b][:, P * z : P * (z + 1)].bitcast(FP8X4),
+                lhsT_scale=ws[b][:, P * z : P * (z + 1)],
+                rhs=gw[z][:, c0:c1].bitcast(FP8X4),
+                rhs_scale=gs[4 * z : P, c0:c1],
+                start=first,
+                stop=not first,
             )
 
-        def evac(b, h, eng):
+        def evac(b, c0, c1, eng, p0=None):
+            p0 = c0 if p0 is None else p0
+            src = acc[b, p0][:, c0 - p0 : c1 - p0]
             if eng == "v":
-                nc.vector.tensor_copy(out=y[b][:, HALF * h : HALF * (h + 1)], in_=acc[b, h][:])
+                nc.vector.tensor_copy(out=y[b][:, c0:c1], in_=src)
             else:
-                nc.scalar.copy(out=y[b][:, HALF * h : HALF * (h + 1)], in_=acc[b, h][:])
-
-        low = [pool.tile([P, V], F32, name=f"low{b}") for b in range(2)]
-        dif = [pool.tile([P, V], F32, name=f"dif{b}") for b in range(2)]
+                nc.scalar.copy(out=y[b][:, c0:c1], in_=src)
 
         def g_lose(b, c0, c1):
             nc.vector.tensor_copy(out=low[b][:, c0:c1], in_=y[b][:].indirect(lose_t[:, c0 // 16 : c1 // 16]))
@@ -97,13 +104,13 @@ def tile_picked_ranknet_sigmoid_p_kernel(tc, x_words, x_scales, w1, offs, win, l
             nc.vector.tensor_tensor(out=dif[b][:, c0:c1], in0=y[b][:].indirect(win_t[:, c0 // 16 : c1 // 16]), in1=low[b][:, c0:c1], op=SUBTRACT)
 
         def finish(b, c0, c1, eng):
-            res = pool.tile([P, c1 - c0], F32, name=f"res{b}{c0}")
+            res = pool.tile([P, c1 - c0], F32, name=f"res{b}_{c0}")
             nc.scalar.activation(out=res[:], in_=dif[b][:, c0:c1], func=SIGMOID)
             eng.dma_start(out=out[P * b : P * (b + 1), c0:c1], in_=res[:])
 
         nc.vector.memset(xs[:].bitcast(I32), 0)
         nc.vector.memset(warm[:], 0.0)
-        load_w(0, 0, nc.sync)
+        load_w(0, 0, 128, nc.sync)
         nc.sync.dma_start(out=offs_t[:], in_=offs)
         load_s(0, nc.sync)
         load_s(1, nc.sync)
@@ -111,37 +118,43 @@ def tile_picked_ranknet_sigmoid_p_kernel(tc, x_words, x_scales, w1, offs, win, l
         load_s(3, nc.sync)
         nc.scalar.activation(out=warm2[:], in_=warm[:], func=SIGMOID)
         load_x(0, nc.sync)
-        load_w(0, 1, nc.sync)
+        load_w(1, 0, 128, nc.sync)
         load_x(1, nc.sync)
-        load_w(1, 0, nc.sync)
-        load_w(1, 1, nc.sync)
+        load_w(0, 128, 256, nc.sync)
+        load_w(1, 128, 256, nc.sync)
         nc.sync.dma_start(out=lose_t[:], in_=lose)
         nc.sync.dma_start(out=win_t[:], in_=win)
-        nc.vector.tensor_copy(out=gs[:], in_=xs[:].indirect(offs_t[:]))
-        cast(0, 0, "s")
-        cast(0, 1, "s")
+        gather_s(0, 512)
         gather_x(0, 0, 512)
+        warm_acc = psum.tile([P, S], F32, name="warm_acc")
+        nc.tensor.matmul_mx(out=warm_acc[:], lhsT=gw[0][:, 0:P].bitcast(FP8X4), lhsT_scale=gs[:, 0:P], rhs=gw[0][:].bitcast(FP8X4), rhs_scale=gs[:], start=True, stop=True)
+        cast(0, 0, 128, "s")
+        cast(1, 0, 128, "s")
         quant(0, 0, 2)
-        mm(0, 0, 0)
-        mm(0, 1, 0)
+        mm(0, 0, 256, 0, True)
+        mm(0, 256, 384, 0, True)
+        mm(0, 384, 512, 0, True)
         gather_x(1, 0, 256)
-        mm(0, 0, 1)
-        gather_x(1, 256, 512)
-        mm(0, 1, 1)
-        cast(1, 0, "s")
-        evac(0, 0, "s")
-        cast(1, 1, "v")
-        evac(0, 1, "s")
+        mm(0, 0, 256, 1, False)
+        gather_x(1, 256, 384)
+        mm(0, 256, 384, 1, False)
+        gather_x(1, 384, 512)
+        mm(0, 384, 512, 1, False)
+        cast(0, 128, 256, "s")
+        evac(0, 0, 256, "s")
+        cast(1, 128, 256, "v")
+        evac(0, 256, 384, "s")
+        evac(0, 384, 512, "s")
         quant(1, 0, 1)
         quant(1, 1, 2)
-        mm(1, 0, 0)
-        mm(1, 1, 0)
-        mm(1, 0, 1)
-        mm(1, 1, 1)
+        mm(1, 0, 256, 0, True)
+        mm(1, 256, 512, 0, True)
+        mm(1, 0, 256, 1, False)
+        mm(1, 256, 512, 1, False)
         g_lose(0, 0, 128)
         g_lose(0, 128, 256)
-        evac(1, 0, "s")
-        evac(1, 1, "s")
+        evac(1, 0, 256, "s")
+        evac(1, 256, 512, "s")
         g_win(0, 0, 128)
         g_win(0, 128, 256)
         finish(0, 0, 256, nc.sync)

@@ -14,6 +14,8 @@ U8 = mybir.dt.uint8
 FP8X4 = mybir.dt.float8_e4m3fn_x4
 SIGMOID = mybir.ActivationFunctionType.Sigmoid
 SUBTRACT = mybir.AluOpType.subtract
+MULT = mybir.AluOpType.mult
+ADD = mybir.AluOpType.add
 
 P = 128
 PACK = 4
@@ -26,114 +28,160 @@ def tile_picked_ranknet_sigmoid_p_kernel(tc, x_words, x_scales, w1, offs, win, l
         pool = ctx.enter_context(tc.tile_pool(name="pool", bufs=1))
         psum = ctx.enter_context(tc.psum_pool(name="psum", bufs=1))
 
+        def new(shape, dtype, name, tag=None):
+            return pool.tile(shape, dtype, name=name, tag=tag or name, align_bytes=64)
+
         offs_t = pool.tile([P, S // 16], U16, name="offs_t")
         win_t = pool.tile([P, V // 16], U16, name="win_t")
         lose_t = pool.tile([P, V // 16], U16, name="lose_t")
-        xs = pool.tile([P, T], U8, name="xs", align_bytes=64)
-        xw = [pool.tile([P, T], I32, name=f"xw{z}", align_bytes=64) for z in range(PASSES)]
-        wbf = [pool.tile([P, PASSES * P * PACK], BF16, name=f"wbf{b}", align_bytes=64) for b in range(2)]
-        wq = [pool.tile([P, PASSES * P], U32, name=f"wq{b}", align_bytes=64) for b in range(2)]
-        ws = [pool.tile([P, PASSES * P], U8, name=f"ws{b}", align_bytes=64) for b in range(2)]
-        gs = pool.tile([P, S], U8, name="gs", align_bytes=64)
-        gw = [pool.tile([P, S], U32, name=f"gw{z}", align_bytes=64) for z in range(PASSES)]
-        y = [pool.tile([P, S], F32, name=f"y{b}", align_bytes=64) for b in range(2)]
-        low = [pool.tile([P, V], F32, name=f"low{b}") for b in range(2)]
-        dif = [pool.tile([P, V], F32, name=f"dif{b}") for b in range(2)]
+        xs = new([P, T], U8, "xs")
         warm = pool.tile([P, 8], F32, name="warm")
         warm2 = pool.tile([P, 8], F32, name="warm2")
-        wraw = []
-        acc = {}
+        xw, wraw, wbf, wq, ws, gw, gs, acc, y, low, dif = {}, {}, {}, {}, {}, {}, {}, {}, {}, {}, {}
 
-        def load_w(z, m0, m1, eng):
-            raw = pool.tile([P, PACK, m1 - m0], F32, name=f"wraw{z}_{m0}", align_bytes=64)
-            wraw.append((z, m0, m1, raw))
+        def find(table, key, c0, c1):
+            a, b, tile = [e for e in table[key] if e[0] <= c0 and c1 <= e[1]][0]
+            return tile, c0 - a, c1 - a
+
+        def load_list(tile, src):
+            nc.sync.dma_start(out=tile[:], in_=src)
+
+        def load_w(z, m0, m1, eng=nc.sync):
+            raw = new([P, PACK, m1 - m0], F32, f"wraw{z}_{m0}")
+            wraw.setdefault(z, []).append((m0, m1, raw))
             eng.dma_start(out=raw[:], in_=w1[512 * z : 512 * (z + 1), m0:m1].rearrange("(p j) m -> p j m", j=PACK))
 
-        def load_x(z, eng):
+        def load_w_split(z, m0, m1, cut, eng):
+            raw = new([P, PACK, m1 - m0], F32, f"wraw{z}_{m0}")
+            wraw.setdefault(z, []).append((m0, m1, raw))
+            rows = w1[512 * z : 512 * (z + 1), m0:m1].rearrange("(p j) m -> p j m", j=PACK)
+            eng.dma_start(out=raw[0:cut], in_=rows[0:cut])
+            eng.dma_start(out=raw[cut:P], in_=rows[cut:P])
+
+        def load_x(z, eng=nc.sync):
+            xw[z] = new([P, T], I32, f"xw{z}")
             eng.dma_start(out=xw[z][:], in_=x_words[z].rearrange("p n t -> p (n t)").bitcast(I32))
 
-        def load_s(q, eng):
+        def load_s(q, eng=nc.sync):
             eng.dma_start(out=xs[32 * q : 32 * q + 8, :].bitcast(I32), in_=x_scales[:, 4 * q : 4 * q + 4, :].bitcast(I32))
 
+        def new_bf(b, z0, z1, tag=None):
+            tile = new([P, (z1 - z0) * P * PACK], BF16, f"wbf{b}_{z0}", tag)
+            for z in range(z0, z1):
+                wbf[b, z] = (tile, z - z0)
+
         def cast(z, m0, m1, eng):
-            zz, a, b, raw = [w for w in wraw if w[0] == z and w[1] <= m0 and m1 <= w[2]][0]
-            c0 = P * z + m0 % P
-            dst = wbf[m0 // P][:, PACK * c0 : PACK * (c0 + m1 - m0)].rearrange("p (c i t) -> p c t i", i=4, t=PACK)
-            src = raw[:, :, m0 - a : m1 - a].rearrange("p t (c i) -> p c t i", i=4)
+            raw, a, b = find(wraw, z, m0, m1)
+            if (m0 // P, z) not in wbf:
+                new_bf(m0 // P, z, z + 1)
+            tile, k = wbf[m0 // P, z]
+            c0 = P * k + m0 % P
+            dst = tile[:, PACK * c0 : PACK * (c0 + m1 - m0)].rearrange("p (c i t) -> p c t i", i=4, t=PACK)
+            src = raw[:, :, a:b].rearrange("p t (c i) -> p c t i", i=4)
             if eng == "v":
                 nc.vector.tensor_copy(out=dst, in_=src)
             elif eng == "g":
-                nc.gpsimd.tensor_copy(out=dst, in_=src)
+                nc.gpsimd.tensor_scalar(out=dst, in0=src, scalar1=1.0, scalar2=0.0, op0=MULT, op1=ADD)
             else:
                 nc.scalar.copy(out=dst, in_=src)
 
-        def quant(b, z0, z1):
-            nc.vector.quantize_mx(out=wq[b][:, P * z0 : P * z1].bitcast(FP8X4), scales=ws[b][:, P * z0 : P * z1], in_=wbf[b][:, PACK * P * z0 : PACK * P * z1])
+        def quant(b, z0, z1, tag_q=None, tag_s=None):
+            tile, k = wbf[b, z0]
+            codes = new([P, (z1 - z0) * P], U32, f"wq{b}_{z0}", tag_q)
+            scales = new([P, (z1 - z0) * P], U8, f"ws{b}_{z0}", tag_s)
+            for z in range(z0, z1):
+                wq[b, z] = codes[:, P * (z - z0) : P * (z - z0 + 1)]
+                ws[b, z] = scales[:, P * (z - z0) : P * (z - z0 + 1)]
+            nc.vector.quantize_mx(out=codes[:].bitcast(FP8X4), scales=scales[:], in_=tile[:, PACK * P * k : PACK * P * (k + z1 - z0)])
+
+        def new_g(table, key, c0, c1, dtype, name, tag=None):
+            table.setdefault(key, []).append((c0, c1, new([P, c1 - c0], dtype, f"{name}{key}_{c0}", tag)))
 
         def gather_s(c0, c1):
-            nc.vector.tensor_copy(out=gs[:, c0:c1], in_=xs[:].indirect(offs_t[:, c0 // 16 : c1 // 16]))
+            tile, a, b = find(gs, 0, c0, c1)
+            nc.vector.tensor_copy(out=tile[:, a:b], in_=xs[:].indirect(offs_t[:, c0 // 16 : c1 // 16]))
 
         def gather_x(z, c0, c1):
-            nc.vector.tensor_copy(out=gw[z][:, c0:c1], in_=xw[z][:].bitcast(U32).indirect(offs_t[:, c0 // 16 : c1 // 16]))
+            tile, a, b = find(gw, z, c0, c1)
+            nc.vector.tensor_copy(out=tile[:, a:b], in_=xw[z][:].bitcast(U32).indirect(offs_t[:, c0 // 16 : c1 // 16]))
 
         def mm(b, c0, c1, z, first):
             if first:
-                acc[b, c0] = psum.tile([P, c1 - c0], F32, name=f"acc{b}_{c0}")
+                acc.setdefault(b, []).append((c0, c1, psum.tile([P, c1 - c0], F32, name=f"acc{b}_{c0}")))
+            bank, a0, a1 = find(acc, b, c0, c1)
+            words, w0, w1c = find(gw, z, c0, c1)
+            scales, s0, s1 = find(gs, 0, c0, c1)
             nc.tensor.matmul_mx(
-                out=acc[b, c0][:],
-                lhsT=wq[b][:, P * z : P * (z + 1)].bitcast(FP8X4),
-                lhsT_scale=ws[b][:, P * z : P * (z + 1)],
-                rhs=gw[z][:, c0:c1].bitcast(FP8X4),
-                rhs_scale=gs[4 * z : P, c0:c1],
+                out=bank[:, a0:a1],
+                lhsT=wq[b, z].bitcast(FP8X4),
+                lhsT_scale=ws[b, z],
+                rhs=words[:, w0:w1c].bitcast(FP8X4),
+                rhs_scale=scales[4 * z : P, s0:s1],
                 start=first,
                 stop=not first,
             )
 
-        def evac(b, c0, c1, eng, p0=None):
-            p0 = c0 if p0 is None else p0
-            src = acc[b, p0][:, c0 - p0 : c1 - p0]
+        def warm_mm(n):
+            bank = psum.tile([P, n], F32, name="warm_acc")
+            words, w0, w1c = find(gw, 0, 0, n)
+            scales, s0, s1 = find(gs, 0, 0, n)
+            nc.tensor.matmul_mx(out=bank[:], lhsT=words[:, w0 : w0 + P].bitcast(FP8X4), lhsT_scale=scales[:, s0 : s0 + P], rhs=words[:, w0:w1c].bitcast(FP8X4), rhs_scale=scales[:, s0:s1], start=True, stop=True)
+
+        def evac(b, c0, c1, eng):
+            if b not in y:
+                y[b] = new([P, S], F32, f"y{b}")
+            bank, a0, a1 = find(acc, b, c0, c1)
             if eng == "v":
-                nc.vector.tensor_copy(out=y[b][:, c0:c1], in_=src)
+                nc.vector.tensor_copy(out=y[b][:, c0:c1], in_=bank[:, a0:a1])
             else:
-                nc.scalar.copy(out=y[b][:, c0:c1], in_=src)
+                nc.scalar.copy(out=y[b][:, c0:c1], in_=bank[:, a0:a1])
 
         def g_lose(b, c0, c1):
+            if b not in low:
+                low[b] = new([P, V], F32, f"low{b}")
             nc.vector.tensor_copy(out=low[b][:, c0:c1], in_=y[b][:].indirect(lose_t[:, c0 // 16 : c1 // 16]))
 
         def g_win(b, c0, c1):
+            if b not in dif:
+                dif[b] = new([P, V], F32, f"dif{b}")
             nc.vector.tensor_tensor(out=dif[b][:, c0:c1], in0=y[b][:].indirect(win_t[:, c0 // 16 : c1 // 16]), in1=low[b][:, c0:c1], op=SUBTRACT)
 
-        def finish(b, c0, c1, eng):
+        def finish(b, c0, c1, eng=nc.sync):
             res = pool.tile([P, c1 - c0], F32, name=f"res{b}_{c0}")
             nc.scalar.activation(out=res[:], in_=dif[b][:, c0:c1], func=SIGMOID)
             eng.dma_start(out=out[P * b : P * (b + 1), c0:c1], in_=res[:])
 
         nc.vector.memset(xs[:].bitcast(I32), 0)
         nc.vector.memset(warm[:], 0.0)
-        load_w(0, 0, 128, nc.sync)
-        nc.sync.dma_start(out=offs_t[:], in_=offs)
-        load_s(0, nc.sync)
-        load_s(1, nc.sync)
-        load_s(2, nc.sync)
-        load_s(3, nc.sync)
+        load_w(0, 0, 128)
+        load_list(offs_t, offs)
+        load_s(0)
+        load_s(1)
+        load_s(2)
+        load_s(3)
         nc.scalar.activation(out=warm2[:], in_=warm[:], func=SIGMOID)
-        load_x(0, nc.sync)
-        load_w(1, 0, 128, nc.sync)
-        load_x(1, nc.sync)
-        load_w(0, 128, 256, nc.sync)
-        load_w(1, 128, 256, nc.sync)
-        nc.sync.dma_start(out=lose_t[:], in_=lose)
-        nc.sync.dma_start(out=win_t[:], in_=win)
+        load_x(0)
+        load_w(1, 0, 128)
+        load_x(1)
+        load_w(0, 128, 256)
+        load_w(1, 128, 256)
+        load_list(lose_t, lose)
+        load_list(win_t, win)
+        new_g(gw, 0, 0, 512, U32, "gw")
+        new_g(gw, 1, 0, 512, U32, "gw")
+        new_g(gs, 0, 0, 512, U8, "gs")
+        cast(0, 0, 128, "v")
+        quant(0, 0, 1)
         gather_s(0, 512)
-        gather_x(0, 0, 512)
-        warm_acc = psum.tile([P, S], F32, name="warm_acc")
-        nc.tensor.matmul_mx(out=warm_acc[:], lhsT=gw[0][:, 0:P].bitcast(FP8X4), lhsT_scale=gs[:, 0:P], rhs=gw[0][:].bitcast(FP8X4), rhs_scale=gs[:], start=True, stop=True)
-        cast(0, 0, 128, "s")
-        cast(1, 0, 128, "s")
-        quant(0, 0, 2)
+        gather_x(0, 0, 256)
         mm(0, 0, 256, 0, True)
+        gather_x(0, 256, 384)
         mm(0, 256, 384, 0, True)
+        gather_x(0, 384, 512)
         mm(0, 384, 512, 0, True)
+        warm_mm(512)
+        cast(1, 0, 128, "s")
+        quant(0, 1, 2)
         gather_x(1, 0, 256)
         mm(0, 0, 256, 1, False)
         gather_x(1, 256, 384)
@@ -157,10 +205,10 @@ def tile_picked_ranknet_sigmoid_p_kernel(tc, x_words, x_scales, w1, offs, win, l
         evac(1, 256, 512, "s")
         g_win(0, 0, 128)
         g_win(0, 128, 256)
-        finish(0, 0, 256, nc.sync)
+        finish(0, 0, 256)
         g_lose(1, 0, 128)
         g_lose(1, 128, 256)
         g_win(1, 0, 128)
-        finish(1, 0, 128, nc.sync)
+        finish(1, 0, 128)
         g_win(1, 128, 256)
-        finish(1, 128, 256, nc.sync)
+        finish(1, 128, 256)

@@ -13,13 +13,13 @@ U16 = mybir.dt.uint16
 U8 = mybir.dt.uint8
 FP8X4 = mybir.dt.float8_e4m3fn_x4
 SIGMOID = mybir.ActivationFunctionType.Sigmoid
+COPY = mybir.ActivationFunctionType.Copy
 SUBTRACT = mybir.AluOpType.subtract
 MULT = mybir.AluOpType.mult
 ADD = mybir.AluOpType.add
 
 P = 128
 PACK = 4
-PASSES = 2
 
 
 def tile_picked_ranknet_sigmoid_p_kernel(tc, x_words, x_scales, w1, offs, win, lose, out):
@@ -31,32 +31,41 @@ def tile_picked_ranknet_sigmoid_p_kernel(tc, x_words, x_scales, w1, offs, win, l
         def new(shape, dtype, name, tag=None):
             return pool.tile(shape, dtype, name=name, tag=tag or name, align_bytes=64)
 
-        offs_t = pool.tile([P, S // 16], U16, name="offs_t")
-        win_t = pool.tile([P, V // 16], U16, name="win_t")
-        lose_t = pool.tile([P, V // 16], U16, name="lose_t")
+        lists = {
+            "offs": pool.tile([P, S // 16], U16, name="offs_t"),
+            "win": pool.tile([P, V // 16], U16, name="win_t"),
+            "lose": pool.tile([P, V // 16], U16, name="lose_t"),
+        }
         xs = new([P, T], U8, "xs")
-        warm = pool.tile([P, 8], F32, name="warm")
-        warm2 = pool.tile([P, 8], F32, name="warm2")
-        xw, wraw, wbf, wq, ws, gw, gs, acc, y, low, dif = {}, {}, {}, {}, {}, {}, {}, {}, {}, {}, {}
+        xw, wraw, wbf, wq, ws, gw, gs, acc, y, got, dif = {}, {}, {}, {}, {}, {}, {}, {}, {}, {}, {}
+
+        res = {}
 
         def find(table, key, c0, c1):
             a, b, tile = [e for e in table[key] if e[0] <= c0 and c1 <= e[1]][0]
-            return tile, c0 - a, c1 - a
+            return tile[:, c0 - a : c1 - a]
 
-        def load_list(tile, src):
-            nc.sync.dma_start(out=tile[:], in_=src)
+        def add(table, key, c0, c1, dtype, name, tag=None):
+            if any(e[0] <= c0 and c1 <= e[1] for e in table.get(key, [])):
+                return
+            table.setdefault(key, []).append((c0, c1, new([P, c1 - c0], dtype, f"{name}_{c0}", tag)))
+
+        def offsets(name, c0, c1):
+            return lists[name][:, c0 // 16 : c1 // 16]
+
+        def warm_sigmoid():
+            warm = pool.tile([P, 8], F32, name="warm")
+            warm2 = pool.tile([P, 8], F32, name="warm2")
+            nc.vector.memset(warm[:], 0.0)
+            nc.scalar.activation(out=warm2[:], in_=warm[:], func=SIGMOID)
+
+        def load_list(name, src):
+            nc.sync.dma_start(out=lists[name][:], in_=src)
 
         def load_w(z, m0, m1, eng=nc.sync):
             raw = new([P, PACK, m1 - m0], F32, f"wraw{z}_{m0}")
             wraw.setdefault(z, []).append((m0, m1, raw))
             eng.dma_start(out=raw[:], in_=w1[512 * z : 512 * (z + 1), m0:m1].rearrange("(p j) m -> p j m", j=PACK))
-
-        def load_w_split(z, m0, m1, cut, eng):
-            raw = new([P, PACK, m1 - m0], F32, f"wraw{z}_{m0}")
-            wraw.setdefault(z, []).append((m0, m1, raw))
-            rows = w1[512 * z : 512 * (z + 1), m0:m1].rearrange("(p j) m -> p j m", j=PACK)
-            eng.dma_start(out=raw[0:cut], in_=rows[0:cut])
-            eng.dma_start(out=raw[cut:P], in_=rows[cut:P])
 
         def load_x(z, eng=nc.sync):
             xw[z] = new([P, T], I32, f"xw{z}")
@@ -65,19 +74,14 @@ def tile_picked_ranknet_sigmoid_p_kernel(tc, x_words, x_scales, w1, offs, win, l
         def load_s(q, eng=nc.sync):
             eng.dma_start(out=xs[32 * q : 32 * q + 8, :].bitcast(I32), in_=x_scales[:, 4 * q : 4 * q + 4, :].bitcast(I32))
 
-        def new_bf(b, z0, z1, tag=None):
-            tile = new([P, (z1 - z0) * P * PACK], BF16, f"wbf{b}_{z0}", tag)
-            for z in range(z0, z1):
-                wbf[b, z] = (tile, z - z0)
-
-        def cast(z, m0, m1, eng):
-            raw, a, b = find(wraw, z, m0, m1)
-            if (m0 // P, z) not in wbf:
-                new_bf(m0 // P, z, z + 1)
-            tile, k = wbf[m0 // P, z]
-            c0 = P * k + m0 % P
-            dst = tile[:, PACK * c0 : PACK * (c0 + m1 - m0)].rearrange("p (c i t) -> p c t i", i=4, t=PACK)
-            src = raw[:, :, a:b].rearrange("p t (c i) -> p c t i", i=4)
+        def cast(z, m0, m1, eng, tag=None):
+            a, b, raw = [e for e in wraw[z] if e[0] <= m0 and m1 <= e[1]][0]
+            g = m0 // P
+            if (g, z) not in wbf:
+                wbf[g, z] = new([P, P * PACK], BF16, f"wbf{g}_{z}", tag)
+            c0 = m0 % P
+            dst = wbf[g, z][:, PACK * c0 : PACK * (c0 + m1 - m0)].rearrange("p (c i t) -> p c t i", i=4, t=PACK)
+            src = raw[:, :, m0 - a : m1 - a].rearrange("p t (c i) -> p c t i", i=4)
             if eng == "v":
                 nc.vector.tensor_copy(out=dst, in_=src)
             elif eng == "g":
@@ -85,130 +89,131 @@ def tile_picked_ranknet_sigmoid_p_kernel(tc, x_words, x_scales, w1, offs, win, l
             else:
                 nc.scalar.copy(out=dst, in_=src)
 
-        def quant(b, z0, z1, tag_q=None, tag_s=None):
-            tile, k = wbf[b, z0]
-            codes = new([P, (z1 - z0) * P], U32, f"wq{b}_{z0}", tag_q)
-            scales = new([P, (z1 - z0) * P], U8, f"ws{b}_{z0}", tag_s)
-            for z in range(z0, z1):
-                wq[b, z] = codes[:, P * (z - z0) : P * (z - z0 + 1)]
-                ws[b, z] = scales[:, P * (z - z0) : P * (z - z0 + 1)]
-            nc.vector.quantize_mx(out=codes[:].bitcast(FP8X4), scales=scales[:], in_=tile[:, PACK * P * k : PACK * P * (k + z1 - z0)])
-
-        def new_g(table, key, c0, c1, dtype, name, tag=None):
-            table.setdefault(key, []).append((c0, c1, new([P, c1 - c0], dtype, f"{name}{key}_{c0}", tag)))
+        def quant(g, z, tag_q=None, tag_s=None):
+            wq[g, z] = new([P, P], U32, f"wq{g}_{z}", tag_q)
+            ws[g, z] = new([P, P], U8, f"ws{g}_{z}", tag_s)
+            nc.vector.quantize_mx(out=wq[g, z][:].bitcast(FP8X4), scales=ws[g, z][:], in_=wbf[g, z][:])
 
         def gather_s(c0, c1):
-            tile, a, b = find(gs, 0, c0, c1)
-            nc.vector.tensor_copy(out=tile[:, a:b], in_=xs[:].indirect(offs_t[:, c0 // 16 : c1 // 16]))
+            nc.vector.tensor_copy(out=find(gs, 0, c0, c1), in_=xs[:].indirect(offsets("offs", c0, c1)))
 
         def gather_x(z, c0, c1):
-            tile, a, b = find(gw, z, c0, c1)
-            nc.vector.tensor_copy(out=tile[:, a:b], in_=xw[z][:].bitcast(U32).indirect(offs_t[:, c0 // 16 : c1 // 16]))
+            nc.vector.tensor_copy(out=find(gw, z, c0, c1), in_=xw[z][:].bitcast(U32).indirect(offsets("offs", c0, c1)))
 
-        def mm(b, c0, c1, z, first):
-            if first:
-                acc.setdefault(b, []).append((c0, c1, psum.tile([P, c1 - c0], F32, name=f"acc{b}_{c0}")))
-            bank, a0, a1 = find(acc, b, c0, c1)
-            words, w0, w1c = find(gw, z, c0, c1)
-            scales, s0, s1 = find(gs, 0, c0, c1)
+        def bank(g, c0, c1):
+            acc.setdefault(g, []).append((c0, c1, psum.tile([P, c1 - c0], F32, name=f"acc{g}_{c0}")))
+
+        def mm(g, c0, c1, z, first, last=None):
+            if last is None:
+                last = not first
+                if first:
+                    bank(g, c0, c1)
             nc.tensor.matmul_mx(
-                out=bank[:, a0:a1],
-                lhsT=wq[b, z].bitcast(FP8X4),
-                lhsT_scale=ws[b, z],
-                rhs=words[:, w0:w1c].bitcast(FP8X4),
-                rhs_scale=scales[4 * z : P, s0:s1],
+                out=find(acc, g, c0, c1),
+                lhsT=wq[g, z][:].bitcast(FP8X4),
+                lhsT_scale=ws[g, z][:],
+                rhs=find(gw, z, c0, c1).bitcast(FP8X4),
+                rhs_scale=find(gs, 0, c0, c1)[4 * z : P, :],
                 start=first,
-                stop=not first,
+                stop=last,
             )
 
-        def warm_mm(n):
-            bank = psum.tile([P, n], F32, name="warm_acc")
-            words, w0, w1c = find(gw, 0, 0, n)
-            scales, s0, s1 = find(gs, 0, 0, n)
-            nc.tensor.matmul_mx(out=bank[:], lhsT=words[:, w0 : w0 + P].bitcast(FP8X4), lhsT_scale=scales[:, s0 : s0 + P], rhs=words[:, w0:w1c].bitcast(FP8X4), rhs_scale=scales[:, s0:s1], start=True, stop=True)
+        def warm_mm(g, z, n):
+            warm_acc = psum.tile([P, n], F32, name=f"warm_acc{n}")
+            nc.tensor.matmul_mx(out=warm_acc[:], lhsT=wq[g, z][:].bitcast(FP8X4), lhsT_scale=ws[g, z][:], rhs=wq[g, z][:, 0:n].bitcast(FP8X4), rhs_scale=ws[g, z][:, 0:n], start=True, stop=True)
 
-        def evac(b, c0, c1, eng):
-            if b not in y:
-                y[b] = new([P, S], F32, f"y{b}")
-            bank, a0, a1 = find(acc, b, c0, c1)
+        def evac(g, c0, c1, eng, tag=None):
+            if g not in y:
+                y[g] = new([P, S], F32, f"y{g}", tag)
             if eng == "v":
-                nc.vector.tensor_copy(out=y[b][:, c0:c1], in_=bank[:, a0:a1])
+                nc.vector.tensor_copy(out=y[g][:, c0:c1], in_=find(acc, g, c0, c1))
             else:
-                nc.scalar.copy(out=y[b][:, c0:c1], in_=bank[:, a0:a1])
+                nc.scalar.copy(out=y[g][:, c0:c1], in_=find(acc, g, c0, c1))
 
-        def g_lose(b, c0, c1):
-            if b not in low:
-                low[b] = new([P, V], F32, f"low{b}")
-            nc.vector.tensor_copy(out=low[b][:, c0:c1], in_=y[b][:].indirect(lose_t[:, c0 // 16 : c1 // 16]))
+        def fetch(name, g, c0, c1, eng, tag=None):
+            add(got, (name, g), c0, c1, F32, f"{name}{g}", tag)
+            window = y[g][:].indirect(offsets(name, c0, c1))
+            if eng == "v":
+                nc.vector.tensor_copy(out=find(got, (name, g), c0, c1), in_=window)
+            else:
+                nc.scalar.activation(out=find(got, (name, g), c0, c1), in_=window, func=COPY)
 
-        def g_win(b, c0, c1):
-            if b not in dif:
-                dif[b] = new([P, V], F32, f"dif{b}")
-            nc.vector.tensor_tensor(out=dif[b][:, c0:c1], in0=y[b][:].indirect(win_t[:, c0 // 16 : c1 // 16]), in1=low[b][:, c0:c1], op=SUBTRACT)
+        def fetch_sub(g, c0, c1, tag=None):
+            add(dif, g, c0, c1, F32, f"dif{g}", tag)
+            nc.vector.tensor_tensor(out=find(dif, g, c0, c1), in0=y[g][:].indirect(offsets("win", c0, c1)), in1=find(got, ("lose", g), c0, c1), op=SUBTRACT)
 
-        def finish(b, c0, c1, eng=nc.sync):
-            res = pool.tile([P, c1 - c0], F32, name=f"res{b}_{c0}")
-            nc.scalar.activation(out=res[:], in_=dif[b][:, c0:c1], func=SIGMOID)
-            eng.dma_start(out=out[P * b : P * (b + 1), c0:c1], in_=res[:])
+        def sub(g, c0, c1, eng="v", tag=None):
+            add(dif, g, c0, c1, F32, f"dif{g}", tag)
+            engine = nc.vector if eng == "v" else nc.gpsimd
+            engine.tensor_tensor(out=find(dif, g, c0, c1), in0=find(got, ("win", g), c0, c1), in1=find(got, ("lose", g), c0, c1), op=SUBTRACT)
+
+        def sigmoid(g, c0, c1):
+            add(res, g, c0, c1, F32, f"res{g}")
+            nc.scalar.activation(out=find(res, g, c0, c1), in_=find(dif, g, c0, c1), func=SIGMOID)
+
+        def store(g, c0, c1, eng=nc.sync):
+            eng.dma_start(out=out[P * g : P * (g + 1), c0:c1], in_=find(res, g, c0, c1))
+
+        def finish(g, c0, c1, eng=nc.sync, tag=None):
+            add(res, g, c0, c1, F32, f"res{g}", tag)
+            sigmoid(g, c0, c1)
+            store(g, c0, c1, eng)
 
         nc.vector.memset(xs[:].bitcast(I32), 0)
-        nc.vector.memset(warm[:], 0.0)
-        load_w(0, 0, 128)
-        load_list(offs_t, offs)
-        load_s(0)
-        load_s(1)
-        load_s(2)
-        load_s(3)
-        nc.scalar.activation(out=warm2[:], in_=warm[:], func=SIGMOID)
-        load_x(0)
         load_w(1, 0, 128)
+        load_list("offs", offs)
+        for q in range(4):
+            load_s(q)
+        warm_sigmoid()
+        load_x(0)
+        load_w(0, 0, 128)
         load_x(1)
         load_w(0, 128, 256)
         load_w(1, 128, 256)
-        load_list(lose_t, lose)
-        load_list(win_t, win)
-        new_g(gw, 0, 0, 512, U32, "gw")
-        new_g(gw, 1, 0, 512, U32, "gw")
-        new_g(gs, 0, 0, 512, U8, "gs")
-        cast(0, 0, 128, "v")
-        quant(0, 0, 1)
+        load_list("lose", lose)
+        load_list("win", win)
+        add(gw, 0, 0, 512, U32, "gw0")
+        add(gw, 1, 0, 512, U32, "gw1")
+        add(gs, 0, 0, 512, U8, "gs")
+        RANGES = [(0, 256), (256, 384), (384, 512)]
+        cast(1, 0, 128, "v")
+        quant(0, 1)
         gather_s(0, 512)
-        gather_x(0, 0, 256)
-        mm(0, 0, 256, 0, True)
-        gather_x(0, 256, 384)
-        mm(0, 256, 384, 0, True)
-        gather_x(0, 384, 512)
-        mm(0, 384, 512, 0, True)
-        warm_mm(512)
-        cast(1, 0, 128, "s")
-        quant(0, 1, 2)
-        gather_x(1, 0, 256)
-        mm(0, 0, 256, 1, False)
-        gather_x(1, 256, 384)
-        mm(0, 256, 384, 1, False)
-        gather_x(1, 384, 512)
-        mm(0, 384, 512, 1, False)
+        gather_x(0, 0, 512)
+        cast(0, 0, 128, "s")
+        quant(0, 0)
+        for c0, c1 in RANGES:
+            mm(0, c0, c1, 0, True)
+        for c0, c1 in RANGES:
+            gather_x(1, c0, c1)
+            mm(0, c0, c1, 1, False)
         cast(0, 128, 256, "s")
-        evac(0, 0, 256, "s")
-        cast(1, 128, 256, "v")
+        cast(1, 128, 192, "s")
+        cast(1, 192, 256, "v")
+        quant(1, 0)
+        evac(0, 0, 256, "v", tag="wraw0_128")
         evac(0, 256, 384, "s")
         evac(0, 384, 512, "s")
-        quant(1, 0, 1)
-        quant(1, 1, 2)
-        mm(1, 0, 256, 0, True)
-        mm(1, 256, 512, 0, True)
-        mm(1, 0, 256, 1, False)
-        mm(1, 256, 512, 1, False)
-        g_lose(0, 0, 128)
-        g_lose(0, 128, 256)
-        evac(1, 0, 256, "s")
-        evac(1, 256, 512, "s")
-        g_win(0, 0, 128)
-        g_win(0, 128, 256)
-        finish(0, 0, 256)
-        g_lose(1, 0, 128)
-        g_lose(1, 128, 256)
-        g_win(1, 0, 128)
+        quant(1, 1)
+        for z in range(2):
+            for c0, c1 in RANGES:
+                mm(1, c0, c1, z, z == 0)
+        for c0 in (0, 128):
+            fetch("lose", 0, c0, c0 + 128, "s")
+            fetch("win", 0, c0, c0 + 128, "v")
+        sub(0, 0, 128)
+        sub(0, 128, 256)
+        evac(1, 0, 256, "s", tag="wraw0_128")
+        evac(1, 256, 384, "v")
+        evac(1, 384, 512, "v")
+        add(res, 0, 0, 256, F32, "res0")
+        sigmoid(0, 0, 128)
+        sigmoid(0, 128, 256)
+        store(0, 0, 256)
+        for c0 in (0, 128):
+            fetch("lose", 1, c0, c0 + 128, "s")
+            fetch("win", 1, c0, c0 + 128, "v")
+        sub(1, 0, 128)
+        sub(1, 128, 256)
         finish(1, 0, 128)
-        g_win(1, 128, 256)
         finish(1, 128, 256)

@@ -188,32 +188,29 @@ def tile_picked_ranknet_sigmoid_p_kernel(tc, x_words, x_scales, w1, offs, win, l
             gather_x(1, c0, c1)
             mm(0, c0, c1, 1, False)
         cast(0, 128, 256, "s")
-        cast(1, 128, 192, "s")
-        cast(1, 192, 256, "v")
+        cast(1, 128, 256, "v")
+        for c0, c1 in RANGES:
+            evac(0, c0, c1, "s")
         quant(1, 0)
-        evac(0, 0, 256, "v", tag="wraw0_128")
-        evac(0, 256, 384, "s")
-        evac(0, 384, 512, "s")
         quant(1, 1)
         for z in range(2):
             for c0, c1 in RANGES:
                 mm(1, c0, c1, z, z == 0)
-        for c0 in (0, 128):
-            fetch("lose", 0, c0, c0 + 128, "s")
-            fetch("win", 0, c0, c0 + 128, "v")
+        add(dif, 0, 0, 256, F32, "dif0")
+        fetch("lose", 0, 0, 128, "s")
+        fetch("lose", 0, 128, 256, "v")
+        fetch("win", 0, 0, 128, "v")
+        fetch_sub(0, 128, 256)
         sub(0, 0, 128)
-        sub(0, 128, 256)
-        evac(1, 0, 256, "s", tag="wraw0_128")
-        evac(1, 256, 384, "v")
-        evac(1, 384, 512, "v")
-        add(res, 0, 0, 256, F32, "res0")
-        sigmoid(0, 0, 128)
-        sigmoid(0, 128, 256)
-        store(0, 0, 256)
-        for c0 in (0, 128):
-            fetch("lose", 1, c0, c0 + 128, "s")
-            fetch("win", 1, c0, c0 + 128, "v")
+        for c0, c1 in RANGES:
+            evac(1, c0, c1, "s")
+        add(got, ("lose", 1), 128, 256, F32, "lose1")
+        fetch("lose", 1, 128, 192, "s")
+        fetch("lose", 1, 192, 256, "v")
+        fetch("lose", 1, 0, 128, "s")
+        fetch("win", 1, 0, 128, "v")
+        fetch_sub(1, 128, 256)
         sub(1, 0, 128)
-        sub(1, 128, 256)
-        finish(1, 0, 128)
+        finish(0, 0, 256, tag="wq1_1")
         finish(1, 128, 256)
+        finish(1, 0, 128)

@@ -100,8 +100,8 @@ def tile_picked_ranknet_sigmoid_p_kernel(tc, x_words, x_scales, w1, offs, win, l
         def gather_x(z, c0, c1):
             nc.vector.tensor_copy(out=find(gw, z, c0, c1), in_=xw[z][:].bitcast(U32).indirect(offsets("offs", c0, c1)))
 
-        def bank(g, c0, c1):
-            acc.setdefault(g, []).append((c0, c1, psum.tile([P, c1 - c0], F32, name=f"acc{g}_{c0}")))
+        def bank(g, c0, c1, tag=None):
+            acc.setdefault(g, []).append((c0, c1, psum.tile([P, c1 - c0], F32, name=f"acc{g}_{c0}", tag=tag or f"acc{g}_{c0}")))
 
         def mm(g, c0, c1, z, first, last=None):
             if last is None:
@@ -193,9 +193,10 @@ def tile_picked_ranknet_sigmoid_p_kernel(tc, x_words, x_scales, w1, offs, win, l
             evac(0, c0, c1, "s")
         quant(1, 0)
         quant(1, 1)
-        for z in range(2):
-            for c0, c1 in RANGES:
-                mm(1, c0, c1, z, z == 0)
+        for c0, c1 in RANGES:
+            order = (0, 1) if c0 == 0 else (1, 0)
+            for z in order:
+                mm(1, c0, c1, z, z == order[0])
         add(dif, 0, 0, 256, F32, "dif0")
         fetch("lose", 0, 0, 128, "s")
         fetch("lose", 0, 128, 256, "v")

@@ -184,26 +184,30 @@ def tile_picked_ranknet_sigmoid_p_kernel(tc, x_words, x_scales, w1, offs, win, l
         quant(0, 0)
         for c0, c1 in RANGES:
             mm(0, c0, c1, 0, True)
+        cast(0, 128, 208, "s")
+        cast(0, 208, 256, "g")
         for c0, c1 in RANGES:
             gather_x(1, c0, c1)
             mm(0, c0, c1, 1, False)
-        cast(0, 128, 256, "s")
-        cast(1, 128, 256, "v")
+        quant(1, 0)
+        cast(1, 128, 256, "v", tag="wraw0_128")
         for c0, c1 in RANGES:
             evac(0, c0, c1, "s")
-        quant(1, 0)
         quant(1, 1)
-        for c0, c1 in RANGES:
-            order = (0, 1) if c0 == 0 else (1, 0)
-            for z in order:
-                mm(1, c0, c1, z, z == order[0])
+        QUARTERS = [(c, c + 128) for c in range(0, S, 128)]
+        for z in range(2):
+            for c0, c1 in QUARTERS:
+                mm(1, c0, c1, z, z == 0)
         add(dif, 0, 0, 256, F32, "dif0")
         fetch("lose", 0, 0, 128, "s")
+        pair = new([P, 256], F32, "pair0", "wraw1_128")
+        got["lose", 0].append((128, 256, pair[:, 0:128]))
+        got["win", 0] = [(0, 128, pair[:, 128:256])]
         fetch("lose", 0, 128, 256, "v")
         fetch("win", 0, 0, 128, "v")
         fetch_sub(0, 128, 256)
         sub(0, 0, 128)
-        for c0, c1 in RANGES:
+        for c0, c1 in QUARTERS:
             evac(1, c0, c1, "s")
         add(got, ("lose", 1), 128, 256, F32, "lose1")
         fetch("lose", 1, 128, 192, "s")

@@ -190,9 +190,11 @@ def tile_picked_ranknet_sigmoid_p_kernel(tc, x_words, x_scales, w1, offs, win, l
             gather_x(1, c0, c1)
             mm(0, c0, c1, 1, False)
         quant(1, 0)
-        cast(1, 128, 256, "v", tag="wraw0_128")
-        for c0, c1 in RANGES:
-            evac(0, c0, c1, "s")
+        cast(1, 128, 192, "v", tag="wraw0_128")
+        cast(1, 192, 256, "s")
+        evac(0, 256, 384, "v", tag="wbf1_0")
+        evac(0, 0, 256, "s")
+        evac(0, 384, 512, "s")
         quant(1, 1)
         QUARTERS = [(c, c + 128) for c in range(0, S, 128)]
         for z in range(2):

@@ -184,8 +184,8 @@ def tile_picked_ranknet_sigmoid_p_kernel(tc, x_words, x_scales, w1, offs, win, l
         quant(0, 0)
         for c0, c1 in RANGES:
             mm(0, c0, c1, 0, True)
-        cast(0, 128, 208, "s")
-        cast(0, 208, 256, "g")
+        cast(0, 128, 224, "s")
+        cast(0, 224, 256, "g")
         for c0, c1 in RANGES:
             gather_x(1, c0, c1)
             mm(0, c0, c1, 1, False)
@@ -218,6 +218,6 @@ def tile_picked_ranknet_sigmoid_p_kernel(tc, x_words, x_scales, w1, offs, win, l
         fetch("win", 1, 0, 128, "v")
         fetch_sub(1, 128, 256)
         sub(1, 0, 128)
-        finish(0, 0, 256, tag="wq1_1")
+        finish(0, 0, 256, nc.scalar, tag="wq1_1")
         finish(1, 128, 256)
         finish(1, 0, 128)

@@ -218,6 +218,6 @@ def tile_picked_ranknet_sigmoid_p_kernel(tc, x_words, x_scales, w1, offs, win, l
         fetch("win", 1, 0, 128, "v")
         fetch_sub(1, 128, 256)
         sub(1, 0, 128)
-        finish(0, 0, 256, nc.scalar, tag="wq1_1")
+        finish(0, 0, 256, tag="wq1_1")
         finish(1, 128, 256)
         finish(1, 0, 128)

@@ -29,7 +29,7 @@ def tile_picked_ranknet_sigmoid_p_kernel(tc, x_words, x_scales, w1, offs, win, l
         psum = ctx.enter_context(tc.psum_pool(name="psum", bufs=1))
 
         def new(shape, dtype, name, tag=None):
-            return pool.tile(shape, dtype, name=name, tag=tag or name, align_bytes=64)
+            return pool.tile(shape, dtype, name=name, tag=tag or name, align_bytes=256)
 
         lists = {
             "offs": pool.tile([P, S // 16], U16, name="offs_t"),

@@ -20,6 +20,7 @@ ADD = mybir.AluOpType.add
 
 P = 128
 PACK = 4
+ALIGN = 256
 
 
 def tile_picked_ranknet_sigmoid_p_kernel(tc, x_words, x_scales, w1, offs, win, lose, out):
@@ -28,18 +29,20 @@ def tile_picked_ranknet_sigmoid_p_kernel(tc, x_words, x_scales, w1, offs, win, l
         pool = ctx.enter_context(tc.tile_pool(name="pool", bufs=1))
         psum = ctx.enter_context(tc.psum_pool(name="psum", bufs=1))
 
+        shared = ctx.enter_context(tc.tile_pool(name="shared", bufs=1))
+
         def new(shape, dtype, name, tag=None):
-            return pool.tile(shape, dtype, name=name, tag=tag or name, align_bytes=256)
+            if isinstance(tag, int):
+                return shared.tile(shape, dtype, name=name, offset=tag, align_bytes=ALIGN)
+            return pool.tile(shape, dtype, name=name, tag=tag or name, align_bytes=ALIGN)
 
         lists = {
-            "offs": pool.tile([P, S // 16], U16, name="offs_t"),
-            "win": pool.tile([P, V // 16], U16, name="win_t"),
-            "lose": pool.tile([P, V // 16], U16, name="lose_t"),
+            "offs": new([P, S // 16], U16, "offs_t"),
+            "win": new([P, V // 16], U16, "win_t"),
+            "lose": new([P, V // 16], U16, "lose_t"),
         }
         xs = new([P, T], U8, "xs")
-        xw, wraw, wbf, wq, ws, gw, gs, acc, y, got, dif = {}, {}, {}, {}, {}, {}, {}, {}, {}, {}, {}
-
-        res = {}
+        xw, wraw, wbf, wq, ws, gw, gs, acc, y, got, dif, res = {}, {}, {}, {}, {}, {}, {}, {}, {}, {}, {}, {}
 
         def find(table, key, c0, c1):
             a, b, tile = [e for e in table[key] if e[0] <= c0 and c1 <= e[1]][0]
@@ -62,17 +65,17 @@ def tile_picked_ranknet_sigmoid_p_kernel(tc, x_words, x_scales, w1, offs, win, l
         def load_list(name, src):
             nc.sync.dma_start(out=lists[name][:], in_=src)
 
-        def load_w(z, m0, m1, eng=nc.sync):
-            raw = new([P, PACK, m1 - m0], F32, f"wraw{z}_{m0}")
+        def load_w(z, m0, m1, tag=None):
+            raw = new([P, PACK, m1 - m0], F32, f"wraw{z}_{m0}", tag)
             wraw.setdefault(z, []).append((m0, m1, raw))
-            eng.dma_start(out=raw[:], in_=w1[512 * z : 512 * (z + 1), m0:m1].rearrange("(p j) m -> p j m", j=PACK))
+            nc.sync.dma_start(out=raw[:], in_=w1[512 * z : 512 * (z + 1), m0:m1].rearrange("(p j) m -> p j m", j=PACK))
 
-        def load_x(z, eng=nc.sync):
+        def load_x(z):
             xw[z] = new([P, T], I32, f"xw{z}")
-            eng.dma_start(out=xw[z][:], in_=x_words[z].rearrange("p n t -> p (n t)").bitcast(I32))
+            nc.sync.dma_start(out=xw[z][:], in_=x_words[z].rearrange("p n t -> p (n t)").bitcast(I32))
 
-        def load_s(q, eng=nc.sync):
-            eng.dma_start(out=xs[32 * q : 32 * q + 8, :].bitcast(I32), in_=x_scales[:, 4 * q : 4 * q + 4, :].bitcast(I32))
+        def load_s(q):
+            nc.sync.dma_start(out=xs[32 * q : 32 * q + 8, :].bitcast(I32), in_=x_scales[:, 4 * q : 4 * q + 4, :].bitcast(I32))
 
         def cast(z, m0, m1, eng, tag=None):
             a, b, raw = [e for e in wraw[z] if e[0] <= m0 and m1 <= e[1]][0]
@@ -100,14 +103,9 @@ def tile_picked_ranknet_sigmoid_p_kernel(tc, x_words, x_scales, w1, offs, win, l
         def gather_x(z, c0, c1):
             nc.vector.tensor_copy(out=find(gw, z, c0, c1), in_=xw[z][:].bitcast(U32).indirect(offsets("offs", c0, c1)))
 
-        def bank(g, c0, c1, tag=None):
-            acc.setdefault(g, []).append((c0, c1, psum.tile([P, c1 - c0], F32, name=f"acc{g}_{c0}", tag=tag or f"acc{g}_{c0}")))
-
-        def mm(g, c0, c1, z, first, last=None):
-            if last is None:
-                last = not first
-                if first:
-                    bank(g, c0, c1)
+        def mm(g, c0, c1, z, first):
+            if first:
+                acc.setdefault(g, []).append((c0, c1, psum.tile([P, c1 - c0], F32, name=f"acc{g}_{c0}")))
             nc.tensor.matmul_mx(
                 out=find(acc, g, c0, c1),
                 lhsT=wq[g, z][:].bitcast(FP8X4),
@@ -115,12 +113,8 @@ def tile_picked_ranknet_sigmoid_p_kernel(tc, x_words, x_scales, w1, offs, win, l
                 rhs=find(gw, z, c0, c1).bitcast(FP8X4),
                 rhs_scale=find(gs, 0, c0, c1)[4 * z : P, :],
                 start=first,
-                stop=last,
+                stop=not first,
             )
-
-        def warm_mm(g, z, n):
-            warm_acc = psum.tile([P, n], F32, name=f"warm_acc{n}")
-            nc.tensor.matmul_mx(out=warm_acc[:], lhsT=wq[g, z][:].bitcast(FP8X4), lhsT_scale=ws[g, z][:], rhs=wq[g, z][:, 0:n].bitcast(FP8X4), rhs_scale=ws[g, z][:, 0:n], start=True, stop=True)
 
         def evac(g, c0, c1, eng, tag=None):
             if g not in y:
@@ -147,17 +141,14 @@ def tile_picked_ranknet_sigmoid_p_kernel(tc, x_words, x_scales, w1, offs, win, l
             engine = nc.vector if eng == "v" else nc.gpsimd
             engine.tensor_tensor(out=find(dif, g, c0, c1), in0=find(got, ("win", g), c0, c1), in1=find(got, ("lose", g), c0, c1), op=SUBTRACT)
 
-        def sigmoid(g, c0, c1):
-            add(res, g, c0, c1, F32, f"res{g}")
-            nc.scalar.activation(out=find(res, g, c0, c1), in_=find(dif, g, c0, c1), func=SIGMOID)
-
-        def store(g, c0, c1, eng=nc.sync):
-            eng.dma_start(out=out[P * g : P * (g + 1), c0:c1], in_=find(res, g, c0, c1))
-
-        def finish(g, c0, c1, eng=nc.sync, tag=None):
+        def finish(g, c0, c1, tag=None):
             add(res, g, c0, c1, F32, f"res{g}", tag)
-            sigmoid(g, c0, c1)
-            store(g, c0, c1, eng)
+            nc.scalar.activation(out=find(res, g, c0, c1), in_=find(dif, g, c0, c1), func=SIGMOID)
+            nc.sync.dma_start(out=out[P * g : P * (g + 1), c0:c1], in_=find(res, g, c0, c1))
+
+        def clock(ap, name):
+            tick = pool.tile([P, 1], ap.dtype, name=name)
+            nc.gpsimd.tensor_copy(out=tick[:], in_=ap)
 
         nc.vector.memset(xs[:].bitcast(I32), 0)
         load_w(1, 0, 128)
@@ -168,14 +159,16 @@ def tile_picked_ranknet_sigmoid_p_kernel(tc, x_words, x_scales, w1, offs, win, l
         load_x(0)
         load_w(0, 0, 128)
         load_x(1)
-        load_w(0, 128, 256)
+        load_w(0, 128, 256, tag=0)
         load_w(1, 128, 256)
         load_list("lose", lose)
         load_list("win", win)
         add(gw, 0, 0, 512, U32, "gw0")
-        add(gw, 1, 0, 512, U32, "gw1")
         add(gs, 0, 0, 512, U8, "gs")
         RANGES = [(0, 256), (256, 384), (384, 512)]
+        for c0, c1 in RANGES:
+            add(gw, 1, c0, c1, U32, "gw1")
+        QUARTERS = [(c, c + 128) for c in range(0, S, 128)]
         cast(1, 0, 128, "v")
         quant(0, 1)
         gather_s(0, 512)
@@ -190,27 +183,27 @@ def tile_picked_ranknet_sigmoid_p_kernel(tc, x_words, x_scales, w1, offs, win, l
             gather_x(1, c0, c1)
             mm(0, c0, c1, 1, False)
         quant(1, 0)
-        cast(1, 128, 192, "v", tag="wraw0_128")
+        cast(1, 128, 192, "v", tag=0)
         cast(1, 192, 256, "s")
-        evac(0, 256, 384, "v", tag="wbf1_0")
+        evac(0, 256, 384, "v", tag=1024)
         evac(0, 0, 256, "s")
         evac(0, 384, 512, "s")
         quant(1, 1)
-        QUARTERS = [(c, c + 128) for c in range(0, S, 128)]
+        TURNS = [QUARTERS[0], QUARTERS[2], QUARTERS[1], QUARTERS[3]]
         for z in range(2):
-            for c0, c1 in QUARTERS:
+            for c0, c1 in TURNS:
                 mm(1, c0, c1, z, z == 0)
-        add(dif, 0, 0, 256, F32, "dif0")
+        add(dif, 0, 0, 256, F32, "dif0", "gw1_256")
         fetch("lose", 0, 0, 128, "s")
         pair = new([P, 256], F32, "pair0", "wraw1_128")
         got["lose", 0].append((128, 256, pair[:, 0:128]))
         got["win", 0] = [(0, 128, pair[:, 128:256])]
         fetch("lose", 0, 128, 256, "v")
         fetch("win", 0, 0, 128, "v")
+        for c0, c1 in TURNS:
+            evac(1, c0, c1, "v" if c0 == 256 else "s")
         fetch_sub(0, 128, 256)
-        sub(0, 0, 128)
-        for c0, c1 in QUARTERS:
-            evac(1, c0, c1, "s")
+        sub(0, 0, 128, "g")
         add(got, ("lose", 1), 128, 256, F32, "lose1")
         fetch("lose", 1, 128, 192, "s")
         fetch("lose", 1, 192, 256, "v")

from contextlib import ExitStack

import concourse.mybir as mybir

K, T, S, V, N = 1024, 1024, 512, 256, 256
FLOPS = 2 * K * S * N

F32 = mybir.dt.float32
BF16 = mybir.dt.bfloat16
I32 = mybir.dt.int32
U32 = mybir.dt.uint32
U16 = mybir.dt.uint16
U8 = mybir.dt.uint8
FP8X4 = mybir.dt.float8_e4m3fn_x4
SIGMOID = mybir.ActivationFunctionType.Sigmoid
COPY = mybir.ActivationFunctionType.Copy
SUBTRACT = mybir.AluOpType.subtract
MULT = mybir.AluOpType.mult
ADD = mybir.AluOpType.add

P = 128
PACK = 4
ALIGN = 256


def tile_picked_ranknet_sigmoid_p_kernel(tc, x_words, x_scales, w1, offs, win, lose, out):
    nc = tc.nc
    with ExitStack() as ctx:
        pool = ctx.enter_context(tc.tile_pool(name="pool", bufs=1))
        psum = ctx.enter_context(tc.psum_pool(name="psum", bufs=1))

        shared = ctx.enter_context(tc.tile_pool(name="shared", bufs=1))

        def new(shape, dtype, name, tag=None):
            if isinstance(tag, int):
                return shared.tile(shape, dtype, name=name, offset=tag, align_bytes=ALIGN)
            return pool.tile(shape, dtype, name=name, tag=tag or name, align_bytes=ALIGN)

        lists = {
            "offs": new([P, S // 16], U16, "offs_t"),
            "win": new([P, V // 16], U16, "win_t"),
            "lose": new([P, V // 16], U16, "lose_t"),
        }
        xs = new([P, T], U8, "xs")
        xw, wraw, wbf, wq, ws, gw, gs, acc, y, got, dif, res = {}, {}, {}, {}, {}, {}, {}, {}, {}, {}, {}, {}

        def find(table, key, c0, c1):
            a, b, tile = [e for e in table[key] if e[0] <= c0 and c1 <= e[1]][0]
            return tile[:, c0 - a : c1 - a]

        def add(table, key, c0, c1, dtype, name, tag=None):
            if any(e[0] <= c0 and c1 <= e[1] for e in table.get(key, [])):
                return
            table.setdefault(key, []).append((c0, c1, new([P, c1 - c0], dtype, f"{name}_{c0}", tag)))

        def offsets(name, c0, c1):
            return lists[name][:, c0 // 16 : c1 // 16]

        def warm_sigmoid():
            warm = pool.tile([P, 8], F32, name="warm")
            warm2 = pool.tile([P, 8], F32, name="warm2")
            nc.vector.memset(warm[:], 0.0)
            nc.scalar.activation(out=warm2[:], in_=warm[:], func=SIGMOID)

        def load_list(name, src):
            nc.sync.dma_start(out=lists[name][:], in_=src)

        def load_w(z, m0, m1, tag=None):
            raw = new([P, PACK, m1 - m0], F32, f"wraw{z}_{m0}", tag)
            wraw.setdefault(z, []).append((m0, m1, raw))
            nc.sync.dma_start(out=raw[:], in_=w1[512 * z : 512 * (z + 1), m0:m1].rearrange("(p j) m -> p j m", j=PACK))

        def load_x(z):
            xw[z] = new([P, T], I32, f"xw{z}")
            nc.sync.dma_start(out=xw[z][:], in_=x_words[z].rearrange("p n t -> p (n t)").bitcast(I32))

        def load_s(q):
            nc.sync.dma_start(out=xs[32 * q : 32 * q + 8, :].bitcast(I32), in_=x_scales[:, 4 * q : 4 * q + 4, :].bitcast(I32))

        def cast(z, m0, m1, eng, tag=None):
            a, b, raw = [e for e in wraw[z] if e[0] <= m0 and m1 <= e[1]][0]
            g = m0 // P
            if (g, z) not in wbf:
                wbf[g, z] = new([P, P * PACK], BF16, f"wbf{g}_{z}", tag)
            c0 = m0 % P
            dst = wbf[g, z][:, PACK * c0 : PACK * (c0 + m1 - m0)].rearrange("p (c i t) -> p c t i", i=4, t=PACK)
            src = raw[:, :, m0 - a : m1 - a].rearrange("p t (c i) -> p c t i", i=4)
            if eng == "v":
                nc.vector.tensor_copy(out=dst, in_=src)
            elif eng == "g":
                nc.gpsimd.tensor_scalar(out=dst, in0=src, scalar1=1.0, scalar2=0.0, op0=MULT, op1=ADD)
            else:
                nc.scalar.copy(out=dst, in_=src)

        def quant(g, z, tag_q=None, tag_s=None):
            wq[g, z] = new([P, P], U32, f"wq{g}_{z}", tag_q)
            ws[g, z] = new([P, P], U8, f"ws{g}_{z}", tag_s)
            nc.vector.quantize_mx(out=wq[g, z][:].bitcast(FP8X4), scales=ws[g, z][:], in_=wbf[g, z][:])

        def gather_s(c0, c1):
            nc.vector.tensor_copy(out=find(gs, 0, c0, c1), in_=xs[:].indirect(offsets("offs", c0, c1)))

        def gather_x(z, c0, c1):
            nc.vector.tensor_copy(out=find(gw, z, c0, c1), in_=xw[z][:].bitcast(U32).indirect(offsets("offs", c0, c1)))

        def mm(g, c0, c1, z, first):
            if first:
                acc.setdefault(g, []).append((c0, c1, psum.tile([P, c1 - c0], F32, name=f"acc{g}_{c0}")))
            nc.tensor.matmul_mx(
                out=find(acc, g, c0, c1),
                lhsT=wq[g, z][:].bitcast(FP8X4),
                lhsT_scale=ws[g, z][:],
                rhs=find(gw, z, c0, c1).bitcast(FP8X4),
                rhs_scale=find(gs, 0, c0, c1)[4 * z : P, :],
                start=first,
                stop=not first,
            )

        def evac(g, c0, c1, eng, tag=None):
            if g not in y:
                y[g] = new([P, S], F32, f"y{g}", tag)
            if eng == "v":
                nc.vector.tensor_copy(out=y[g][:, c0:c1], in_=find(acc, g, c0, c1))
            else:
                nc.scalar.copy(out=y[g][:, c0:c1], in_=find(acc, g, c0, c1))

        def fetch(name, g, c0, c1, eng, tag=None):
            add(got, (name, g), c0, c1, F32, f"{name}{g}", tag)
            window = y[g][:].indirect(offsets(name, c0, c1))
            if eng == "v":
                nc.vector.tensor_copy(out=find(got, (name, g), c0, c1), in_=window)
            else:
                nc.scalar.activation(out=find(got, (name, g), c0, c1), in_=window, func=COPY)

        def fetch_sub(g, c0, c1, tag=None):
            add(dif, g, c0, c1, F32, f"dif{g}", tag)
            nc.vector.tensor_tensor(out=find(dif, g, c0, c1), in0=y[g][:].indirect(offsets("win", c0, c1)), in1=find(got, ("lose", g), c0, c1), op=SUBTRACT)

        def sub(g, c0, c1, eng="v", tag=None):
            add(dif, g, c0, c1, F32, f"dif{g}", tag)
            engine = nc.vector if eng == "v" else nc.gpsimd
            engine.tensor_tensor(out=find(dif, g, c0, c1), in0=find(got, ("win", g), c0, c1), in1=find(got, ("lose", g), c0, c1), op=SUBTRACT)

        def finish(g, c0, c1, tag=None):
            add(res, g, c0, c1, F32, f"res{g}", tag)
            nc.scalar.activation(out=find(res, g, c0, c1), in_=find(dif, g, c0, c1), func=SIGMOID)
            nc.sync.dma_start(out=out[P * g : P * (g + 1), c0:c1], in_=find(res, g, c0, c1))

        def clock(ap, name):
            tick = pool.tile([P, 1], ap.dtype, name=name)
            nc.gpsimd.tensor_copy(out=tick[:], in_=ap)

        nc.vector.memset(xs[:].bitcast(I32), 0)
        load_w(1, 0, 128)
        load_list("offs", offs)
        for q in range(4):
            load_s(q)
        warm_sigmoid()
        load_x(0)
        load_w(0, 0, 128)
        load_x(1)
        load_w(0, 128, 256, tag=0)
        load_w(1, 128, 256)
        load_list("lose", lose)
        load_list("win", win)
        add(gw, 0, 0, 512, U32, "gw0")
        add(gs, 0, 0, 512, U8, "gs")
        RANGES = [(0, 256), (256, 384), (384, 512)]
        for c0, c1 in RANGES:
            add(gw, 1, c0, c1, U32, "gw1")
        QUARTERS = [(c, c + 128) for c in range(0, S, 128)]
        cast(1, 0, 128, "v")
        quant(0, 1)
        gather_s(0, 512)
        gather_x(0, 0, 512)
        cast(0, 0, 128, "s")
        quant(0, 0)
        for c0, c1 in RANGES:
            mm(0, c0, c1, 0, True)
        cast(0, 128, 224, "s")
        cast(0, 224, 256, "g")
        for c0, c1 in RANGES:
            gather_x(1, c0, c1)
            mm(0, c0, c1, 1, False)
        quant(1, 0)
        cast(1, 128, 192, "v", tag=0)
        cast(1, 192, 256, "s")
        evac(0, 256, 384, "v", tag=1024)
        evac(0, 0, 256, "s")
        evac(0, 384, 512, "s")
        quant(1, 1)
        TURNS = [QUARTERS[0], QUARTERS[2], QUARTERS[1], QUARTERS[3]]
        for z in range(2):
            for c0, c1 in TURNS:
                mm(1, c0, c1, z, z == 0)
        add(dif, 0, 0, 256, F32, "dif0", "gw1_256")
        fetch("lose", 0, 0, 128, "s")
        pair = new([P, 256], F32, "pair0", "wraw1_128")
        got["lose", 0].append((128, 256, pair[:, 0:128]))
        got["win", 0] = [(0, 128, pair[:, 128:256])]
        fetch("lose", 0, 128, 256, "v")
        fetch("win", 0, 0, 128, "v")
        for c0, c1 in TURNS:
            evac(1, c0, c1, "v" if c0 == 256 else "s")
        fetch_sub(0, 128, 256)
        sub(0, 0, 128, "g")
        add(got, ("lose", 1), 128, 256, F32, "lose1")
        fetch("lose", 1, 128, 192, "s")
        fetch("lose", 1, 192, 256, "v")
        fetch("lose", 1, 0, 128, "s")
        fetch("win", 1, 0, 128, "v")
        fetch_sub(1, 128, 256)
        sub(1, 0, 128)
        finish(0, 0, 256, tag="wq1_1")
        finish(1, 128, 256)
        finish(1, 0, 128)
